import numpy as np
import ml_dtypes


def mxq(x, axis, fmt="e4m3"):
    dtype, down = {"e4m3": (ml_dtypes.float8_e4m3fn, 7), "e5m2": (ml_dtypes.float8_e5m2, 14)}[fmt]
    v = np.moveaxis(np.asarray(x, np.float32).astype(ml_dtypes.bfloat16).astype(np.float64), axis, -1)
    blocks = v.reshape(v.shape[:-1] + (-1, 32))
    amax = np.abs(blocks).max(-1, keepdims=True)
    byte = np.maximum(np.where(amax > 0, np.frexp(amax)[1] - 1 + 127, 0) - down, 1)
    scale = np.exp2(byte - 127.0)
    codes = (blocks / scale).astype(np.float32).astype(dtype).astype(np.float64)
    return np.moveaxis((codes * scale).reshape(v.shape), -1, axis)


WIDE = False


def mx_kscale(k):
    if not WIDE:
        return np.ones(k)
    levels = np.array([10, -10, 5, -5, 0])
    if k % 512:
        return np.exp2(np.random.permutation(np.resize(levels, k // 32))).repeat(32)
    a = np.empty((k // 512, 16))
    for p in range(k // 512):
        a[p, :8] = np.random.permutation(np.resize(levels, 8))
        for g in range(8):
            far = levels[np.abs(levels - a[p, g]) >= 10]
            a[p, g + 8] = far[np.random.randint(len(far))]
    return np.exp2(a.ravel()).repeat(32)


def f64(x):
    return np.asarray(x).astype(np.float64)


def striped(idx):
    return np.tile(idx.reshape(-1, 16).T, (8, 1)).astype(np.uint16)


def unstriped(offs):
    return offs[:16].T.reshape(-1).astype(np.int64)


def pack_weight(w):
    k, n = w.shape
    w = f64(np.asarray(w, np.float32).astype(ml_dtypes.bfloat16)).reshape(k // 32, 32, n)
    amax = np.abs(w).max(1)
    byte = np.clip(np.where(amax > 0, np.frexp(amax)[1] - 1 + 127 - 7, 1), 1, 254)
    scaled = (w * np.exp2(127.0 - byte)[:, None, :]).reshape(k, n).astype(np.float32)
    words = np.ascontiguousarray(scaled.reshape(k // 512, 128, 4, n).transpose(0, 1, 3, 2)).astype(ml_dtypes.float8_e4m3fn).view(np.uint8)
    return words, np.ascontiguousarray(byte.astype(np.uint8).reshape(k // 512, 16, n))


def unpack_weight(words, scales):
    g, p, n, _ = words.shape
    vals = np.ascontiguousarray(words).view(ml_dtypes.float8_e4m3fn).astype(np.float64) * np.repeat(np.exp2(scales.astype(np.float64) - 127.0), 8, axis=1)[..., None]
    return vals.transpose(0, 1, 3, 2).reshape(g * 512, n)


def relu(v):
    return np.maximum(v, 0.0)


K, T, S, N = 512, 2048, 512, 256


def setup_inputs():
    n = np.random.standard_normal
    s = mx_kscale(K)[:, None]
    packed_xT = pack_weight(n((K, T)) * s)
    return {
        "x_words": packed_xT[0],
        "x_scales": packed_xT[1],
        "w1": (n((K, N)) / np.sqrt(K) / s).astype(np.float32),
        "offs": striped(np.random.permutation(T)[:S]),
        "style": striped(np.random.permutation(T)[:S]),
    }


def reference(x_words, x_scales, w1, offs, style):
    xq = unpack_weight(x_words, x_scales)[:, unstriped(offs)]
    w1q = mxq(f64(w1), 0, "e4m3")
    y = w1q.T @ xq
    my = y.mean(axis=1, keepdims=True)
    dy = y - my
    x_style = unpack_weight(x_words, x_scales)[:, unstriped(style)]
    z = w1q.T @ x_style
    mz = z.mean(axis=1, keepdims=True)
    dz = z - mz
    qz = (dz) ** 2
    sz = np.sqrt(qz.mean(axis=1, keepdims=True) + 1e-4)
    qy = (dy) ** 2
    sy = np.sqrt(qy.mean(axis=1, keepdims=True) + 1e-4)
    f = sz / sy
    return relu(dy * f + mz)

@@ -1,0 +1,119 @@
+from contextlib import ExitStack
+
+import concourse.mybir as mybir
+
+K, T, S, N = 512, 2048, 512, 256
+EPS = 1e-4
+FLOPS = 2 * 2 * K * N * S
+
+F32 = mybir.dt.float32
+BF16 = mybir.dt.bfloat16
+I32 = mybir.dt.int32
+U32 = mybir.dt.uint32
+U16 = mybir.dt.uint16
+U8 = mybir.dt.uint8
+FP8X4 = mybir.dt.float8_e4m3fn_x4
+ACT = mybir.ActivationFunctionType
+ALU = mybir.AluOpType
+
+P = 128
+PACK = 4
+HALF = S // 2
+LIST_COLS = S // 16
+
+
+def tile_picked_yadain_relu_p_kernel(tc, x_words, x_scales, w1, offs, style, out):
+    nc = tc.nc
+    with ExitStack() as ctx:
+        sb = ctx.enter_context(tc.tile_pool(name="sb", bufs=1))
+        ps = ctx.enter_context(tc.psum_pool(name="ps", bufs=1))
+
+        content_list = sb.tile([P, LIST_COLS], U16, name="content_list")
+        style_list = sb.tile([P, LIST_COLS], U16, name="style_list")
+        nc.sync.dma_start(content_list[:], offs)
+        nc.sync.dma_start(style_list[:], style)
+
+        scale_table = sb.tile([P, T], U8, name="scale_table", tag="table_then_codes", align_bytes=64)
+        nc.vector.memset(scale_table[:].bitcast(I32), 0)
+        for q in range(4):
+            nc.sync.dma_start(scale_table[32 * q : 32 * q + 4, :].bitcast(I32), x_scales[0, 4 * q : 4 * q + 4, :].bitcast(I32))
+
+        w_raw = sb.tile([P, PACK, N], F32, name="w_raw", align_bytes=64)
+        nc.scalar.dma_start(w_raw[:], w1.rearrange("(p j) m -> p j m", j=PACK))
+        word_table = sb.tile([P, T], I32, name="word_table", align_bytes=64)
+        nc.scalar.dma_start(word_table[:], x_words[0].rearrange("p n t -> p (n t)").bitcast(I32))
+
+        warm_in = sb.tile([P, 1], F32, name="warm_in")
+        warm_out = sb.tile([P, 1], F32, name="warm_out")
+        nc.vector.memset(warm_in[:], 1.0)
+        nc.scalar.activation(warm_out[:], warm_in[:], ACT.Sqrt)
+
+        w_bf = sb.tile([P, N, PACK], BF16, name="w_bf", tag="weights_then_words", align_bytes=64)
+        nc.scalar.copy(
+            w_bf[:].rearrange("p (c i) t -> p c t i", i=4),
+            w_raw[:].rearrange("p t (c i) -> p c t i", i=4),
+        )
+
+        y_scales = sb.tile([P, S], U8, name="y_scales", align_bytes=64)
+        z_scales = sb.tile([P, S], U8, name="z_scales", align_bytes=64)
+        nc.vector.tensor_copy(y_scales[:], scale_table[:].indirect(content_list[:]))
+        nc.vector.tensor_copy(z_scales[:], scale_table[:].indirect(style_list[:]))
+
+        w_codes = sb.tile([P, N], U32, name="w_codes", tag="table_then_codes", align_bytes=64)
+        w_scales = sb.tile([P, N], U8, name="w_scales", align_bytes=64)
+        nc.vector.quantize_mx(w_codes[:].bitcast(FP8X4), w_scales[:], w_bf[:].rearrange("p m t -> p (m t)"))
+
+        y = [ps.tile([P, S], F32, name="y%d" % b) for b in range(2)]
+        z = [ps.tile([P, S], F32, name="z%d" % b) for b in range(2)]
+        picked = sb.tile([P, 2 * S], U32, name="picked", tag="weights_then_words", align_bytes=64)
+        for first, picks, scales, banks in ((0, content_list, y_scales, y), (S, style_list, z_scales, z)):
+            for h in range(2):
+                words = picked[:, first + h * HALF : first + (h + 1) * HALF]
+                cols = slice(h * HALF, (h + 1) * HALF)
+                nc.vector.tensor_copy(
+                    words, word_table[:].bitcast(U32).indirect(picks[:, h * HALF // 16 : (h + 1) * HALF // 16])
+                )
+                for b in range(2):
+                    rows = slice(b * P, (b + 1) * P)
+                    nc.tensor.matmul_mx(
+                        banks[b][:, cols],
+                        lhsT=w_codes[:, rows].bitcast(FP8X4),
+                        lhsT_scale=w_scales[:, rows],
+                        rhs=words.bitcast(FP8X4),
+                        rhs_scale=scales[:, cols],
+                        start=True,
+                        stop=True,
+                    )
+
+        neg_my = [sb.tile([P, 1], F32, name="neg_my%d" % b) for b in range(2)]
+        var_y = [sb.tile([P, 1], F32, name="var_y%d" % b) for b in range(2)]
+        spare = sb.tile([P, S], BF16, name="spare")
+        sq_sum = sb.tile([P, 1], F32, name="sq_sum")
+        nc.scalar.activation(spare[:], y[0][:], ACT.Copy, scale=-1.0 / S, accum_out=neg_my[0][:])
+        nc.scalar.activation(spare[:], y[0][:], ACT.Square, bias=neg_my[0][:], accum_out=sq_sum[:])
+        nc.scalar.activation(var_y[0][:], sq_sum[:], ACT.Identity, scale=1.0 / S, bias=EPS)
+
+        def stats(bank, name):
+            parts = sb.tile([P, 6], F32, name=name + "_parts")
+            mv = sb.tile([P, 2], F32, name=name + "_mv")
+            nc.vector.bn_stats(parts[:], bank[:])
+            nc.vector.bn_aggr(mv[:], parts[:])
+            return mv
+
+        y1 = stats(y[1], "y1")
+        nc.scalar.activation(var_y[1][:], y1[:, 1:2], ACT.Identity, bias=EPS)
+        nc.scalar.activation(neg_my[1][:], y1[:, 0:1], ACT.Copy, scale=-1.0)
+
+        for b in range(2):
+            inv = sb.tile([P, 1], F32, name="inv%d" % b)
+            inv_eps = sb.tile([P, 1], F32, name="inv_eps%d" % b)
+            nc.vector.reciprocal(inv[:], var_y[b][:])
+            nc.scalar.activation(inv_eps[:], inv[:], ACT.Copy, scale=EPS)
+            zs = stats(z[b], "z%d" % b)
+            f = sb.tile([P, 1], F32, name="f%d" % b)
+            shift = sb.tile([P, 1], F32, name="shift%d" % b)
+            nc.scalar.activation(f[:], zs[:, 1:2], ACT.Sqrt, scale=inv[:], bias=inv_eps[:])
+            nc.scalar.activation(shift[:], f[:], ACT.Identity, scale=neg_my[b][:], bias=zs[:, 0:1])
+            res = sb.tile([P, S], F32, name="res%d" % b)
+            nc.scalar.activation(res[:], y[b][:], ACT.Relu, scale=f[:], bias=shift[:])
+            nc.sync.dma_start(out[b * P : (b + 1) * P, :], res[:])

@@ -20,6 +20,7 @@ P = 128
 PACK = 4
 HALF = S // 2
 LIST_COLS = S // 16
+LEAD = 512
 
 
 def tile_picked_yadain_relu_p_kernel(tc, x_words, x_scales, w1, offs, style, out):
@@ -33,22 +34,24 @@ def tile_picked_yadain_relu_p_kernel(tc, x_words, x_scales, w1, offs, style, out
         nc.sync.dma_start(content_list[:], offs)
         nc.sync.dma_start(style_list[:], style)
 
-        scale_table = sb.tile([P, T], U8, name="scale_table", tag="table_then_codes", align_bytes=64)
+        scale_table = sb.tile([P, T], U8, name="scale_table", align_bytes=64)
         nc.vector.memset(scale_table[:].bitcast(I32), 0)
-        for q in range(4):
-            nc.sync.dma_start(scale_table[32 * q : 32 * q + 4, :].bitcast(I32), x_scales[0, 4 * q : 4 * q + 4, :].bitcast(I32))
-
-        w_raw = sb.tile([P, PACK, N], F32, name="w_raw", align_bytes=64)
-        nc.scalar.dma_start(w_raw[:], w1.rearrange("(p j) m -> p j m", j=PACK))
         word_table = sb.tile([P, T], I32, name="word_table", align_bytes=64)
-        nc.scalar.dma_start(word_table[:], x_words[0].rearrange("p n t -> p (n t)").bitcast(I32))
+        hbm_words = x_words[0].rearrange("p n t -> p (n t)").bitcast(I32)
+        nc.sync.dma_start(word_table[:, :LEAD], hbm_words[:, :LEAD])
+        for q in range(4):
+            queue = nc.sync if q < 2 else nc.scalar
+            queue.dma_start(scale_table[32 * q : 32 * q + 4, :].bitcast(I32), x_scales[0, 4 * q : 4 * q + 4, :].bitcast(I32))
+        w_raw = sb.tile([P, PACK, N], F32, name="w_raw", align_bytes=64)
+        nc.sync.dma_start(w_raw[:], w1.rearrange("(p j) m -> p j m", j=PACK))
+        nc.sync.dma_start(word_table[:, LEAD:], hbm_words[:, LEAD:])
 
         warm_in = sb.tile([P, 1], F32, name="warm_in")
         warm_out = sb.tile([P, 1], F32, name="warm_out")
         nc.vector.memset(warm_in[:], 1.0)
         nc.scalar.activation(warm_out[:], warm_in[:], ACT.Sqrt)
 
-        w_bf = sb.tile([P, N, PACK], BF16, name="w_bf", tag="weights_then_words", align_bytes=64)
+        w_bf = sb.tile([P, N, PACK], BF16, name="w_bf", align_bytes=64)
         nc.scalar.copy(
             w_bf[:].rearrange("p (c i) t -> p c t i", i=4),
             w_raw[:].rearrange("p t (c i) -> p c t i", i=4),
@@ -59,61 +62,83 @@ def tile_picked_yadain_relu_p_kernel(tc, x_words, x_scales, w1, offs, style, out
         nc.vector.tensor_copy(y_scales[:], scale_table[:].indirect(content_list[:]))
         nc.vector.tensor_copy(z_scales[:], scale_table[:].indirect(style_list[:]))
 
-        w_codes = sb.tile([P, N], U32, name="w_codes", tag="table_then_codes", align_bytes=64)
+        w_codes = sb.tile([P, N], U32, name="w_codes", align_bytes=64)
         w_scales = sb.tile([P, N], U8, name="w_scales", align_bytes=64)
         nc.vector.quantize_mx(w_codes[:].bitcast(FP8X4), w_scales[:], w_bf[:].rearrange("p m t -> p (m t)"))
 
-        y = [ps.tile([P, S], F32, name="y%d" % b) for b in range(2)]
-        z = [ps.tile([P, S], F32, name="z%d" % b) for b in range(2)]
-        picked = sb.tile([P, 2 * S], U32, name="picked", tag="weights_then_words", align_bytes=64)
-        for first, picks, scales, banks in ((0, content_list, y_scales, y), (S, style_list, z_scales, z)):
-            for h in range(2):
-                words = picked[:, first + h * HALF : first + (h + 1) * HALF]
-                cols = slice(h * HALF, (h + 1) * HALF)
-                nc.vector.tensor_copy(
-                    words, word_table[:].bitcast(U32).indirect(picks[:, h * HALF // 16 : (h + 1) * HALF // 16])
-                )
-                for b in range(2):
-                    rows = slice(b * P, (b + 1) * P)
-                    nc.tensor.matmul_mx(
-                        banks[b][:, cols],
-                        lhsT=w_codes[:, rows].bitcast(FP8X4),
-                        lhsT_scale=w_scales[:, rows],
-                        rhs=words.bitcast(FP8X4),
-                        rhs_scale=scales[:, cols],
-                        start=True,
-                        stop=True,
-                    )
+        y_words = sb.tile([P, S], U32, name="y_words", align_bytes=64)
+        z_words = sb.tile([P, S], U32, name="z_words", align_bytes=64)
+        y0 = ps.tile([P, S], F32, name="y0")
+        y1 = [ps.tile([P, HALF], F32, name="y1_%d" % h) for h in range(2)]
+        z = [[ps.tile([P, HALF], F32, name="z%d_%d" % (b, h)) for h in range(2)] for b in range(2)]
+        halves = [slice(0, HALF), slice(HALF, S)]
 
-        neg_my = [sb.tile([P, 1], F32, name="neg_my%d" % b) for b in range(2)]
-        var_y = [sb.tile([P, 1], F32, name="var_y%d" % b) for b in range(2)]
-        spare = sb.tile([P, S], BF16, name="spare")
-        sq_sum = sb.tile([P, 1], F32, name="sq_sum")
-        nc.scalar.activation(spare[:], y[0][:], ACT.Copy, scale=-1.0 / S, accum_out=neg_my[0][:])
-        nc.scalar.activation(spare[:], y[0][:], ACT.Square, bias=neg_my[0][:], accum_out=sq_sum[:])
-        nc.scalar.activation(var_y[0][:], sq_sum[:], ACT.Identity, scale=1.0 / S, bias=EPS)
+        def gather_words(words, picks, cols):
+            offsets = picks[:, cols.start // 16 : cols.stop // 16]
+            nc.vector.tensor_copy(words[:, cols], word_table[:].bitcast(U32).indirect(offsets))
 
-        def stats(bank, name):
-            parts = sb.tile([P, 6], F32, name=name + "_parts")
-            mv = sb.tile([P, 2], F32, name=name + "_mv")
-            nc.vector.bn_stats(parts[:], bank[:])
-            nc.vector.bn_aggr(mv[:], parts[:])
-            return mv
+        def project(dst, b, words, scales, cols):
+            rows = slice(b * P, (b + 1) * P)
+            nc.tensor.matmul_mx(
+                dst,
+                lhsT=w_codes[:, rows].bitcast(FP8X4),
+                lhsT_scale=w_scales[:, rows],
+                rhs=words[:, cols].bitcast(FP8X4),
+                rhs_scale=scales[:, cols],
+                start=True,
+                stop=True,
+            )
 
-        y1 = stats(y[1], "y1")
-        nc.scalar.activation(var_y[1][:], y1[:, 1:2], ACT.Identity, bias=EPS)
-        nc.scalar.activation(neg_my[1][:], y1[:, 0:1], ACT.Copy, scale=-1.0)
+        for h, cols in enumerate(halves):
+            gather_words(y_words, content_list, cols)
+            project(y0[:, cols], 0, y_words, y_scales, cols)
+            project(y1[h][:], 1, y_words, y_scales, cols)
+        for h, cols in enumerate(halves):
+            gather_words(z_words, style_list, cols)
+            for b in range(2):
+                project(z[b][h][:], b, z_words, z_scales, cols)
 
-        for b in range(2):
-            inv = sb.tile([P, 1], F32, name="inv%d" % b)
-            inv_eps = sb.tile([P, 1], F32, name="inv_eps%d" % b)
-            nc.vector.reciprocal(inv[:], var_y[b][:])
-            nc.scalar.activation(inv_eps[:], inv[:], ACT.Copy, scale=EPS)
-            zs = stats(z[b], "z%d" % b)
-            f = sb.tile([P, 1], F32, name="f%d" % b)
-            shift = sb.tile([P, 1], F32, name="shift%d" % b)
-            nc.scalar.activation(f[:], zs[:, 1:2], ACT.Sqrt, scale=inv[:], bias=inv_eps[:])
-            nc.scalar.activation(shift[:], f[:], ACT.Identity, scale=neg_my[b][:], bias=zs[:, 0:1])
-            res = sb.tile([P, S], F32, name="res%d" % b)
-            nc.scalar.activation(res[:], y[b][:], ACT.Relu, scale=f[:], bias=shift[:])
-            nc.sync.dma_start(out[b * P : (b + 1) * P, :], res[:])
+        def column(name, n=1):
+            return sb.tile([P, n], F32, name=name)
+
+        y0_small = sb.tile([P, S], F32, name="y0_small")
+        squares = sb.tile([P, S], BF16, name="squares")
+        my0, sq_sum, my0_small, neg_my1 = column("my0"), column("sq_sum"), column("my0_small"), column("neg_my1")
+        denom, inv, inv_eps1 = column("denom", 2), column("inv", 2), column("inv_eps1")
+        parts = [column("parts%d" % i, 12) for i in range(3)]
+        y1_mv, z0_mv, z1_mv = column("y1_mv", 2), column("z0_mv", 2), column("z1_mv", 2)
+        sz0, f0, f1 = column("sz0"), column("f0"), column("f1")
+        dy1 = sb.tile([P, S], F32, name="dy1")
+
+        nc.scalar.activation(y0_small[:], y0[:], ACT.Copy, scale=1.0 / S, accum_out=my0[:])
+        nc.scalar.activation(squares[:], y0[:], ACT.Square, scale=-1.0, bias=my0[:], accum_out=sq_sum[:])
+        for h in range(2):
+            nc.vector.bn_stats(parts[0][:, 6 * h : 6 * h + 6], y1[h][:])
+        nc.vector.bn_stats(parts[1][:, 0:6], z[0][0][:])
+        nc.vector.bn_aggr(y1_mv[:], parts[0][:])
+        nc.vector.bn_stats(parts[2][:, 0:6], z[1][0][:])
+        nc.vector.bn_stats(parts[1][:, 6:12], z[0][1][:])
+        nc.scalar.activation(neg_my1[:], y1_mv[:, 0:1], ACT.Copy, scale=-1.0)
+        nc.scalar.activation(denom[:, 1:2], y1_mv[:, 1:2], ACT.Identity, bias=EPS)
+        nc.scalar.activation(denom[:, 0:1], sq_sum[:], ACT.Sqrt, scale=1.0 / S**3, bias=EPS / S**2)
+        nc.scalar.activation(my0_small[:], my0[:], ACT.Copy, scale=1.0 / S)
+        nc.vector.bn_aggr(z0_mv[:], parts[1][:])
+        nc.vector.bn_stats(parts[2][:, 6:12], z[1][1][:])
+        nc.vector.reciprocal(inv[:], denom[:])
+        nc.vector.bn_aggr(z1_mv[:], parts[2][:])
+        nc.scalar.activation(sz0[:], z0_mv[:, 1:2], ACT.Sqrt, bias=EPS)
+        for h, cols in enumerate(halves):
+            nc.scalar.activation(dy1[:, cols], y1[h][:], ACT.Identity, bias=neg_my1[:])
+        nc.scalar.activation(inv_eps1[:], inv[:, 1:2], ACT.Copy, scale=EPS)
+        nc.scalar.activation(f1[:], z1_mv[:, 1:2], ACT.Sqrt, scale=inv[:, 1:2], bias=inv_eps1[:])
+        nc.vector.tensor_tensor(f0[:], sz0[:], inv[:, 0:1], ALU.mult)
+
+        scaled0 = sb.tile([P, S], F32, name="scaled0")
+        res = [[sb.tile([P, HALF], F32, name="res%d_%d" % (b, h)) for h in range(2)] for b in range(2)]
+        for cols in halves:
+            nc.vector.tensor_scalar(scaled0[:, cols], y0_small[:, cols], my0_small[:], f0[:], ALU.subtract, ALU.mult)
+        for h, cols in enumerate(halves):
+            nc.vector.tensor_scalar(res[0][h][:], scaled0[:, cols], z0_mv[:, 0:1], 0.0, ALU.add, ALU.max)
+            nc.sync.dma_start(out[0:P, cols], res[0][h][:])
+            nc.scalar.activation(res[1][h][:], dy1[:, cols], ACT.Relu, scale=f1[:], bias=z1_mv[:, 0:1])
+            nc.sync.dma_start(out[P : 2 * P, cols], res[1][h][:])

@@ -41,7 +41,7 @@ def tile_picked_yadain_relu_p_kernel(tc, x_words, x_scales, w1, offs, style, out
         nc.sync.dma_start(word_table[:, :LEAD], hbm_words[:, :LEAD])
         for q in range(4):
             queue = nc.sync if q < 2 else nc.scalar
-            queue.dma_start(scale_table[32 * q : 32 * q + 4, :].bitcast(I32), x_scales[0, 4 * q : 4 * q + 4, :].bitcast(I32))
+            queue.dma_start(scale_table[q:P:32, :].bitcast(I32), x_scales[0, q:16:4, :].bitcast(I32))
         w_raw = sb.tile([P, PACK, N], F32, name="w_raw", align_bytes=64)
         nc.sync.dma_start(w_raw[:], w1.rearrange("(p j) m -> p j m", j=PACK))
         nc.sync.dma_start(word_table[:, LEAD:], hbm_words[:, LEAD:])
@@ -104,10 +104,10 @@ def tile_picked_yadain_relu_p_kernel(tc, x_words, x_scales, w1, offs, style, out
         y0_small = sb.tile([P, S], F32, name="y0_small")
         squares = sb.tile([P, S], BF16, name="squares")
         my0, sq_sum, my0_small, neg_my1 = column("my0"), column("sq_sum"), column("my0_small"), column("neg_my1")
-        denom, inv, inv_eps1 = column("denom", 2), column("inv", 2), column("inv_eps1")
+        denom, inv, inv_eps1 = [column("sy0"), column("vy1")], [column("inv0"), column("inv1")], column("inv_eps1")
         parts = [column("parts%d" % i, 12) for i in range(3)]
         y1_mv, z0_mv, z1_mv = column("y1_mv", 2), column("z0_mv", 2), column("z1_mv", 2)
-        sz0, f0, f1 = column("sz0"), column("f0"), column("f1")
+        sz0, f1 = column("sz0"), column("f1")
         dy1 = sb.tile([P, S], F32, name="dy1")
 
         nc.scalar.activation(y0_small[:], y0[:], ACT.Copy, scale=1.0 / S, accum_out=my0[:])
@@ -118,27 +118,31 @@ def tile_picked_yadain_relu_p_kernel(tc, x_words, x_scales, w1, offs, style, out
         nc.vector.bn_aggr(y1_mv[:], parts[0][:])
         nc.vector.bn_stats(parts[2][:, 0:6], z[1][0][:])
         nc.vector.bn_stats(parts[1][:, 6:12], z[0][1][:])
+        nc.scalar.activation(denom[1][:], y1_mv[:, 1:2], ACT.Identity, bias=EPS)
         nc.scalar.activation(neg_my1[:], y1_mv[:, 0:1], ACT.Copy, scale=-1.0)
-        nc.scalar.activation(denom[:, 1:2], y1_mv[:, 1:2], ACT.Identity, bias=EPS)
-        nc.scalar.activation(denom[:, 0:1], sq_sum[:], ACT.Sqrt, scale=1.0 / S**3, bias=EPS / S**2)
+        nc.scalar.activation(denom[0][:], sq_sum[:], ACT.Sqrt, scale=1.0 / S**3, bias=EPS / S**2)
         nc.scalar.activation(my0_small[:], my0[:], ACT.Copy, scale=1.0 / S)
+        nc.vector.reciprocal(inv[1][:], denom[1][:])
         nc.vector.bn_aggr(z0_mv[:], parts[1][:])
         nc.vector.bn_stats(parts[2][:, 6:12], z[1][1][:])
-        nc.vector.reciprocal(inv[:], denom[:])
+        nc.vector.reciprocal(inv[0][:], denom[0][:])
         nc.vector.bn_aggr(z1_mv[:], parts[2][:])
         nc.scalar.activation(sz0[:], z0_mv[:, 1:2], ACT.Sqrt, bias=EPS)
         for h, cols in enumerate(halves):
             nc.scalar.activation(dy1[:, cols], y1[h][:], ACT.Identity, bias=neg_my1[:])
-        nc.scalar.activation(inv_eps1[:], inv[:, 1:2], ACT.Copy, scale=EPS)
-        nc.scalar.activation(f1[:], z1_mv[:, 1:2], ACT.Sqrt, scale=inv[:, 1:2], bias=inv_eps1[:])
-        nc.vector.tensor_tensor(f0[:], sz0[:], inv[:, 0:1], ALU.mult)
+        nc.scalar.activation(inv_eps1[:], inv[1][:], ACT.Copy, scale=EPS)
+        nc.scalar.activation(f1[:], z1_mv[:, 1:2], ACT.Sqrt, scale=inv[1][:], bias=inv_eps1[:])
 
-        scaled0 = sb.tile([P, S], F32, name="scaled0")
+        normed0 = sb.tile([P, S], F32, name="normed0")
+        styled0 = sb.tile([P, HALF], F32, name="styled0")
         res = [[sb.tile([P, HALF], F32, name="res%d_%d" % (b, h)) for h in range(2)] for b in range(2)]
         for cols in halves:
-            nc.vector.tensor_scalar(scaled0[:, cols], y0_small[:, cols], my0_small[:], f0[:], ALU.subtract, ALU.mult)
+            nc.vector.tensor_scalar(normed0[:, cols], y0_small[:, cols], my0_small[:], inv[0][:], ALU.subtract, ALU.mult)
+        nc.vector.tensor_scalar(styled0[:], normed0[:, halves[0]], sz0[:], z0_mv[:, 0:1], ALU.mult, ALU.add)
+        nc.vector.tensor_scalar_max(res[0][1][:], styled0[:], 0.0)
+        nc.sync.dma_start(out[0:P, halves[0]], res[0][1][:])
         for h, cols in enumerate(halves):
-            nc.vector.tensor_scalar(res[0][h][:], scaled0[:, cols], z0_mv[:, 0:1], 0.0, ALU.add, ALU.max)
-            nc.sync.dma_start(out[0:P, cols], res[0][h][:])
             nc.scalar.activation(res[1][h][:], dy1[:, cols], ACT.Relu, scale=f1[:], bias=z1_mv[:, 0:1])
             nc.sync.dma_start(out[P : 2 * P, cols], res[1][h][:])
+        nc.scalar.activation(res[0][0][:], normed0[:, halves[1]], ACT.Relu, scale=sz0[:], bias=z0_mv[:, 0:1])
+        nc.sync.dma_start(out[0:P, halves[1]], res[0][0][:])

from contextlib import ExitStack

import concourse.mybir as mybir

K, T, S, N = 512, 2048, 512, 256
EPS = 1e-4
FLOPS = 2 * 2 * K * N * S

F32 = mybir.dt.float32
BF16 = mybir.dt.bfloat16
I32 = mybir.dt.int32
U32 = mybir.dt.uint32
U16 = mybir.dt.uint16
U8 = mybir.dt.uint8
FP8X4 = mybir.dt.float8_e4m3fn_x4
ACT = mybir.ActivationFunctionType
ALU = mybir.AluOpType

P = 128
PACK = 4
HALF = S // 2
LIST_COLS = S // 16
LEAD = 512


def tile_picked_yadain_relu_p_kernel(tc, x_words, x_scales, w1, offs, style, out):
    nc = tc.nc
    with ExitStack() as ctx:
        sb = ctx.enter_context(tc.tile_pool(name="sb", bufs=1))
        ps = ctx.enter_context(tc.psum_pool(name="ps", bufs=1))

        content_list = sb.tile([P, LIST_COLS], U16, name="content_list")
        style_list = sb.tile([P, LIST_COLS], U16, name="style_list")
        nc.sync.dma_start(content_list[:], offs)
        nc.sync.dma_start(style_list[:], style)

        scale_table = sb.tile([P, T], U8, name="scale_table", align_bytes=64)
        nc.vector.memset(scale_table[:].bitcast(I32), 0)
        word_table = sb.tile([P, T], I32, name="word_table", align_bytes=64)
        hbm_words = x_words[0].rearrange("p n t -> p (n t)").bitcast(I32)
        nc.sync.dma_start(word_table[:, :LEAD], hbm_words[:, :LEAD])
        for q in range(4):
            queue = nc.sync if q < 2 else nc.scalar
            queue.dma_start(scale_table[q:P:32, :].bitcast(I32), x_scales[0, q:16:4, :].bitcast(I32))
        w_raw = sb.tile([P, PACK, N], F32, name="w_raw", align_bytes=64)
        nc.sync.dma_start(w_raw[:], w1.rearrange("(p j) m -> p j m", j=PACK))
        nc.sync.dma_start(word_table[:, LEAD:], hbm_words[:, LEAD:])

        warm_in = sb.tile([P, 1], F32, name="warm_in")
        warm_out = sb.tile([P, 1], F32, name="warm_out")
        nc.vector.memset(warm_in[:], 1.0)
        nc.scalar.activation(warm_out[:], warm_in[:], ACT.Sqrt)

        w_bf = sb.tile([P, N, PACK], BF16, name="w_bf", align_bytes=64)
        nc.scalar.copy(
            w_bf[:].rearrange("p (c i) t -> p c t i", i=4),
            w_raw[:].rearrange("p t (c i) -> p c t i", i=4),
        )

        y_scales = sb.tile([P, S], U8, name="y_scales", align_bytes=64)
        z_scales = sb.tile([P, S], U8, name="z_scales", align_bytes=64)
        nc.vector.tensor_copy(y_scales[:], scale_table[:].indirect(content_list[:]))
        nc.vector.tensor_copy(z_scales[:], scale_table[:].indirect(style_list[:]))

        w_codes = sb.tile([P, N], U32, name="w_codes", align_bytes=64)
        w_scales = sb.tile([P, N], U8, name="w_scales", align_bytes=64)
        nc.vector.quantize_mx(w_codes[:].bitcast(FP8X4), w_scales[:], w_bf[:].rearrange("p m t -> p (m t)"))

        y_words = sb.tile([P, S], U32, name="y_words", align_bytes=64)
        z_words = sb.tile([P, S], U32, name="z_words", align_bytes=64)
        y0 = ps.tile([P, S], F32, name="y0")
        y1 = [ps.tile([P, HALF], F32, name="y1_%d" % h) for h in range(2)]
        z = [[ps.tile([P, HALF], F32, name="z%d_%d" % (b, h)) for h in range(2)] for b in range(2)]
        halves = [slice(0, HALF), slice(HALF, S)]

        def gather_words(words, picks, cols):
            offsets = picks[:, cols.start // 16 : cols.stop // 16]
            nc.vector.tensor_copy(words[:, cols], word_table[:].bitcast(U32).indirect(offsets))

        def project(dst, b, words, scales, cols):
            rows = slice(b * P, (b + 1) * P)
            nc.tensor.matmul_mx(
                dst,
                lhsT=w_codes[:, rows].bitcast(FP8X4),
                lhsT_scale=w_scales[:, rows],
                rhs=words[:, cols].bitcast(FP8X4),
                rhs_scale=scales[:, cols],
                start=True,
                stop=True,
            )

        for h, cols in enumerate(halves):
            gather_words(y_words, content_list, cols)
            project(y0[:, cols], 0, y_words, y_scales, cols)
            project(y1[h][:], 1, y_words, y_scales, cols)
        for h, cols in enumerate(halves):
            gather_words(z_words, style_list, cols)
            for b in range(2):
                project(z[b][h][:], b, z_words, z_scales, cols)

        def column(name, n=1):
            return sb.tile([P, n], F32, name=name)

        y0_small = sb.tile([P, S], F32, name="y0_small")
        squares = sb.tile([P, S], BF16, name="squares")
        my0, sq_sum, my0_small, neg_my1 = column("my0"), column("sq_sum"), column("my0_small"), column("neg_my1")
        denom, inv, inv_eps1 = [column("sy0"), column("vy1")], [column("inv0"), column("inv1")], column("inv_eps1")
        parts = [column("parts%d" % i, 12) for i in range(3)]
        y1_mv, z0_mv, z1_mv = column("y1_mv", 2), column("z0_mv", 2), column("z1_mv", 2)
        sz0, f1 = column("sz0"), column("f1")
        dy1 = sb.tile([P, S], F32, name="dy1")

        nc.scalar.activation(y0_small[:], y0[:], ACT.Copy, scale=1.0 / S, accum_out=my0[:])
        nc.scalar.activation(squares[:], y0[:], ACT.Square, scale=-1.0, bias=my0[:], accum_out=sq_sum[:])
        for h in range(2):
            nc.vector.bn_stats(parts[0][:, 6 * h : 6 * h + 6], y1[h][:])
        nc.vector.bn_stats(parts[1][:, 0:6], z[0][0][:])
        nc.vector.bn_aggr(y1_mv[:], parts[0][:])
        nc.vector.bn_stats(parts[2][:, 0:6], z[1][0][:])
        nc.vector.bn_stats(parts[1][:, 6:12], z[0][1][:])
        nc.scalar.activation(denom[1][:], y1_mv[:, 1:2], ACT.Identity, bias=EPS)
        nc.scalar.activation(neg_my1[:], y1_mv[:, 0:1], ACT.Copy, scale=-1.0)
        nc.scalar.activation(denom[0][:], sq_sum[:], ACT.Sqrt, scale=1.0 / S**3, bias=EPS / S**2)
        nc.scalar.activation(my0_small[:], my0[:], ACT.Copy, scale=1.0 / S)
        nc.vector.reciprocal(inv[1][:], denom[1][:])
        nc.vector.bn_aggr(z0_mv[:], parts[1][:])
        nc.vector.bn_stats(parts[2][:, 6:12], z[1][1][:])
        nc.vector.reciprocal(inv[0][:], denom[0][:])
        nc.vector.bn_aggr(z1_mv[:], parts[2][:])
        nc.scalar.activation(sz0[:], z0_mv[:, 1:2], ACT.Sqrt, bias=EPS)
        for h, cols in enumerate(halves):
            nc.scalar.activation(dy1[:, cols], y1[h][:], ACT.Identity, bias=neg_my1[:])
        nc.scalar.activation(inv_eps1[:], inv[1][:], ACT.Copy, scale=EPS)
        nc.scalar.activation(f1[:], z1_mv[:, 1:2], ACT.Sqrt, scale=inv[1][:], bias=inv_eps1[:])

        normed0 = sb.tile([P, S], F32, name="normed0")
        styled0 = sb.tile([P, HALF], F32, name="styled0")
        res = [[sb.tile([P, HALF], F32, name="res%d_%d" % (b, h)) for h in range(2)] for b in range(2)]
        for cols in halves:
            nc.vector.tensor_scalar(normed0[:, cols], y0_small[:, cols], my0_small[:], inv[0][:], ALU.subtract, ALU.mult)
        nc.vector.tensor_scalar(styled0[:], normed0[:, halves[0]], sz0[:], z0_mv[:, 0:1], ALU.mult, ALU.add)
        nc.vector.tensor_scalar_max(res[0][1][:], styled0[:], 0.0)
        nc.sync.dma_start(out[0:P, halves[0]], res[0][1][:])
        for h, cols in enumerate(halves):
            nc.scalar.activation(res[1][h][:], dy1[:, cols], ACT.Relu, scale=f1[:], bias=z1_mv[:, 0:1])
            nc.sync.dma_start(out[P : 2 * P, cols], res[1][h][:])
        nc.scalar.activation(res[0][0][:], normed0[:, halves[1]], ACT.Relu, scale=sz0[:], bias=z0_mv[:, 0:1])
        nc.sync.dma_start(out[0:P, halves[1]], res[0][0][:])
